import numpy as np, ml_dtypes
CORES = [64,65,66,67,68,69,70,71,72,73,74,75,76,77,78,79,80,81,82,83,84,85,86,87,88,89,90,91,92,93,94,95]
N = 32
def setup_inputs(rng):
    return {"x": rng.standard_normal((N, 128, 8), dtype=np.float32).astype(ml_dtypes.bfloat16)}
def reference(x):
    s = x.sum(axis=0, dtype=np.float64).astype(x.dtype)
    s = np.maximum(s, 0)
    return {"y": np.broadcast_to(s, (N,) + s.shape)}

@@ -1,0 +1,88 @@
+from concourse.bass import DstId, RemoteDMATransfer
+from concourse.mybir import AluOpType
+
+W = 8
+SCRATCH = {
+    "land": ("sbuf", [128, 8 * W], "bfloat16"),
+    "t1": ("sbuf", [128, 4 * W], "float32"),
+    "t2": ("sbuf", [128, 2 * W], "float32"),
+    "part": ("sbuf", [128, 4 * W], "bfloat16"),
+    "u1": ("sbuf", [128, 2 * W], "float32"),
+    "u2": ("sbuf", [128, W], "float32"),
+    "zero": ("sbuf", [128, W], "float32"),
+    "ys": ("sbuf", [128, W], "bfloat16"),
+}
+SEMAPHORES = ["ld", "a1", "a2", "sent", "v", "st"]
+
+GATEWAYS = (2, 3, 6, 7)
+PARTNER = {2: 0, 3: 1, 6: 4, 7: 5}
+
+
+def rank_program(g, core, T, topo):
+    rank = T.rank_of(core)
+    if rank is None:
+        return
+    S = T.sem
+    chips = sorted({topo.chip(c) for c in T.cores})
+    ch, k = topo.chip(core), core % 8
+    j = chips.index(ch)
+    gateway = k in GATEWAYS
+    add, vmax = AluOpType.add, AluOpType.max
+
+    def dst(c):
+        rid, pid, _se = topo.addr(c)
+        return DstId(rid=rid, pnc=pid)
+
+    mine = T.land[:, k * W:(k + 1) * W]
+    g.sync.dma_start(mine, T.x[:]).then_inc(S.ld, 16)
+    g.vector.memset(T.zero[:], 0.0).then_inc(S.v, 1)
+    nv = 1
+
+    to = [ch * 8 + q for q in GATEWAYS if q != k]
+    g.wait_ge(S.ld, 16)
+    g.remote_dma_fused(
+        [RemoteDMATransfer(dst_ids=[dst(c) for c in to], dma_engine_mask=0xFFFF, remote_sem=S.a1,
+                           srcs=[mine], dsts=[mine for _c in to])],
+        local_sem=S.sent)
+    sent = 16
+
+    got2 = 4 * 8
+    if gateway:
+        v = g.vector
+        v.wait_ge(S.ld, 16)
+        v.wait_ge(S.a1, 7 * 16)
+        v.tensor_tensor(T.t1[:], T.land[:, 0:4 * W], T.land[:, 4 * W:8 * W], add).then_inc(S.v, 1)
+        nv += 1
+        v.wait_ge(S.v, nv)
+        v.tensor_tensor(T.t2[:], T.t1[:, 0:2 * W], T.t1[:, 2 * W:4 * W], add).then_inc(S.v, 1)
+        nv += 1
+        v.wait_ge(S.v, nv)
+        slot = T.part[:, j * W:(j + 1) * W]
+        v.tensor_tensor(slot, T.t2[:, 0:W], T.t2[:, W:2 * W], add).then_inc(S.v, 1)
+        nv += 1
+        far = [c * 8 + q for c in chips if c != ch for q in (PARTNER[k], k)]
+        g.wait_ge(S.v, nv)
+        g.remote_dma_fused(
+            [RemoteDMATransfer(dst_ids=[dst(c) for c in far], dma_engine_mask=0x00FF, remote_sem=S.a2,
+                               srcs=[slot], dsts=[slot for _c in far]),
+             RemoteDMATransfer(dst_ids=[dst(ch * 8 + PARTNER[k])], dma_engine_mask=0xFF00, remote_sem=S.a2,
+                               srcs=[slot], dsts=[slot])],
+            local_sem=S.sent)
+        sent += 16
+        got2 = 3 * 8
+
+    v = g.vector
+    v.wait_ge(S.v, nv)
+    v.wait_ge(S.a2, got2)
+    v.tensor_tensor(T.u1[:], T.part[:, 0:2 * W], T.part[:, 2 * W:4 * W], add).then_inc(S.v, 1)
+    nv += 1
+    v.wait_ge(S.v, nv)
+    v.tensor_tensor(T.u2[:], T.u1[:, 0:W], T.u1[:, W:2 * W], add).then_inc(S.v, 1)
+    nv += 1
+    v.wait_ge(S.v, nv)
+    v.tensor_tensor(T.ys[:], T.u2[:], T.zero[:], vmax).then_inc(S.v, 1)
+    nv += 1
+    g.sync.wait_ge(S.v, nv)
+    g.sync.dma_start(T.y[:], T.ys[:]).then_inc(S.st, 16)
+    g.sync.wait_ge(S.st, 16)
+    g.wait_ge(S.sent, sent)

@@ -3,12 +3,9 @@ from concourse.mybir import AluOpType
 
 W = 8
 SCRATCH = {
-    "land": ("sbuf", [128, 8 * W], "bfloat16"),
-    "t1": ("sbuf", [128, 4 * W], "float32"),
-    "t2": ("sbuf", [128, 2 * W], "float32"),
-    "part": ("sbuf", [128, 4 * W], "bfloat16"),
-    "u1": ("sbuf", [128, 2 * W], "float32"),
-    "u2": ("sbuf", [128, W], "float32"),
+    "gath": ("dram", [16, 128, W], "bfloat16"),
+    "part": ("sbuf", [128, 2 * W], "bfloat16"),
+    "u": ("sbuf", [128, W], "float32"),
     "zero": ("sbuf", [128, W], "float32"),
     "ys": ("sbuf", [128, W], "bfloat16"),
 }
@@ -16,73 +13,52 @@ SEMAPHORES = ["ld", "a1", "a2", "sent", "v", "st"]
 
 GATEWAYS = (2, 3, 6, 7)
 PARTNER = {2: 0, 3: 1, 6: 4, 7: 5}
+TWIN = {2: 3, 3: 2, 6: 7, 7: 6}
+OFF_CHIP, ON_CHIP = 0x00FF, 0xFF00
 
 
 def rank_program(g, core, T, topo):
-    rank = T.rank_of(core)
-    if rank is None:
+    if T.rank_of(core) is None:
         return
     S = T.sem
-    chips = sorted({topo.chip(c) for c in T.cores})
     ch, k = topo.chip(core), core % 8
-    j = chips.index(ch)
-    gateway = k in GATEWAYS
-    add, vmax = AluOpType.add, AluOpType.max
+    par = ch & 1
+    plane = sorted({topo.chip(c) for c in T.cores if topo.chip(c) & 1 == par})
+    sister = [c for c in plane if c != ch][0]
 
-    def dst(c):
-        rid, pid, _se = topo.addr(c)
-        return DstId(rid=rid, pnc=pid)
+    def ids(cores):
+        return [DstId(rid=topo.addr(c)[0], pnc=topo.addr(c)[1]) for c in cores]
 
-    mine = T.land[:, k * W:(k + 1) * W]
+    def send(far, near, srcs, dst, sem, alu_op):
+        g.remote_dma_fused(
+            [RemoteDMATransfer(dst_ids=ids(far), dma_engine_mask=OFF_CHIP, remote_sem=sem,
+                               srcs=srcs, dsts=[dst for _c in far], alu_op=alu_op),
+             RemoteDMATransfer(dst_ids=ids(near), dma_engine_mask=ON_CHIP, remote_sem=sem,
+                               srcs=srcs, dsts=[dst for _c in near], alu_op=alu_op)],
+            local_sem=S.sent)
+
+    mine = T.gath[8 * plane.index(ch) + k]
     g.sync.dma_start(mine, T.x[:]).then_inc(S.ld, 16)
     g.vector.memset(T.zero[:], 0.0).then_inc(S.v, 1)
-    nv = 1
 
-    to = [ch * 8 + q for q in GATEWAYS if q != k]
     g.wait_ge(S.ld, 16)
-    g.remote_dma_fused(
-        [RemoteDMATransfer(dst_ids=[dst(c) for c in to], dma_engine_mask=0xFFFF, remote_sem=S.a1,
-                           srcs=[mine], dsts=[mine for _c in to])],
-        local_sem=S.sent)
+    send([8 * sister + q for q in GATEWAYS], [8 * ch + q for q in GATEWAYS if q != k], [mine], mine, S.a1, 0)
     sent = 16
 
-    got2 = 4 * 8
-    if gateway:
-        v = g.vector
-        v.wait_ge(S.ld, 16)
-        v.wait_ge(S.a1, 7 * 16)
-        v.tensor_tensor(T.t1[:], T.land[:, 0:4 * W], T.land[:, 4 * W:8 * W], add).then_inc(S.v, 1)
-        nv += 1
-        v.wait_ge(S.v, nv)
-        v.tensor_tensor(T.t2[:], T.t1[:, 0:2 * W], T.t1[:, 2 * W:4 * W], add).then_inc(S.v, 1)
-        nv += 1
-        v.wait_ge(S.v, nv)
-        slot = T.part[:, j * W:(j + 1) * W]
-        v.tensor_tensor(slot, T.t2[:, 0:W], T.t2[:, W:2 * W], add).then_inc(S.v, 1)
-        nv += 1
-        far = [c * 8 + q for c in chips if c != ch for q in (PARTNER[k], k)]
-        g.wait_ge(S.v, nv)
-        g.remote_dma_fused(
-            [RemoteDMATransfer(dst_ids=[dst(c) for c in far], dma_engine_mask=0x00FF, remote_sem=S.a2,
-                               srcs=[slot], dsts=[slot for _c in far]),
-             RemoteDMATransfer(dst_ids=[dst(ch * 8 + PARTNER[k])], dma_engine_mask=0xFF00, remote_sem=S.a2,
-                               srcs=[slot], dsts=[slot])],
-            local_sem=S.sent)
+    if k in GATEWAYS:
+        mate = ch ^ 1
+        g.wait_ge(S.a1, 15 * 8)
+        send([8 * mate + PARTNER[k], 8 * mate + k], [8 * ch + PARTNER[k], 8 * ch + TWIN[k]],
+             [T.gath[i] for i in range(16)], T.part[:, par * W:(par + 1) * W], S.a2, 1)
         sent += 16
-        got2 = 3 * 8
 
     v = g.vector
-    v.wait_ge(S.v, nv)
-    v.wait_ge(S.a2, got2)
-    v.tensor_tensor(T.u1[:], T.part[:, 0:2 * W], T.part[:, 2 * W:4 * W], add).then_inc(S.v, 1)
-    nv += 1
-    v.wait_ge(S.v, nv)
-    v.tensor_tensor(T.u2[:], T.u1[:, 0:W], T.u1[:, W:2 * W], add).then_inc(S.v, 1)
-    nv += 1
-    v.wait_ge(S.v, nv)
-    v.tensor_tensor(T.ys[:], T.u2[:], T.zero[:], vmax).then_inc(S.v, 1)
-    nv += 1
-    g.sync.wait_ge(S.v, nv)
+    v.wait_ge(S.v, 1)
+    v.wait_ge(S.a2, 2 * 8)
+    v.tensor_tensor(T.u[:], T.part[:, 0:W], T.part[:, W:2 * W], AluOpType.add).then_inc(S.v, 1)
+    v.wait_ge(S.v, 2)
+    v.tensor_tensor(T.ys[:], T.u[:], T.zero[:], AluOpType.max).then_inc(S.v, 1)
+    g.sync.wait_ge(S.v, 3)
     g.sync.dma_start(T.y[:], T.ys[:]).then_inc(S.st, 16)
     g.sync.wait_ge(S.st, 16)
     g.wait_ge(S.sent, sent)

from concourse.bass import DstId, RemoteDMATransfer
from concourse.mybir import AluOpType

W = 8
SCRATCH = {
    "gath": ("dram", [16, 128, W], "bfloat16"),
    "part": ("sbuf", [128, 2 * W], "bfloat16"),
    "u": ("sbuf", [128, W], "float32"),
    "zero": ("sbuf", [128, W], "float32"),
    "ys": ("sbuf", [128, W], "bfloat16"),
}
SEMAPHORES = ["ld", "a1", "a2", "sent", "v", "st"]

GATEWAYS = (2, 3, 6, 7)
PARTNER = {2: 0, 3: 1, 6: 4, 7: 5}
TWIN = {2: 3, 3: 2, 6: 7, 7: 6}
OFF_CHIP, ON_CHIP = 0x00FF, 0xFF00


def rank_program(g, core, T, topo):
    if T.rank_of(core) is None:
        return
    S = T.sem
    ch, k = topo.chip(core), core % 8
    par = ch & 1
    plane = sorted({topo.chip(c) for c in T.cores if topo.chip(c) & 1 == par})
    sister = [c for c in plane if c != ch][0]

    def ids(cores):
        return [DstId(rid=topo.addr(c)[0], pnc=topo.addr(c)[1]) for c in cores]

    def send(far, near, srcs, dst, sem, alu_op):
        g.remote_dma_fused(
            [RemoteDMATransfer(dst_ids=ids(far), dma_engine_mask=OFF_CHIP, remote_sem=sem,
                               srcs=srcs, dsts=[dst for _c in far], alu_op=alu_op),
             RemoteDMATransfer(dst_ids=ids(near), dma_engine_mask=ON_CHIP, remote_sem=sem,
                               srcs=srcs, dsts=[dst for _c in near], alu_op=alu_op)],
            local_sem=S.sent)

    mine = T.gath[8 * plane.index(ch) + k]
    g.sync.dma_start(mine, T.x[:]).then_inc(S.ld, 16)
    g.vector.memset(T.zero[:], 0.0).then_inc(S.v, 1)

    g.wait_ge(S.ld, 16)
    send([8 * sister + q for q in GATEWAYS], [8 * ch + q for q in GATEWAYS if q != k], [mine], mine, S.a1, 0)
    sent = 16

    if k in GATEWAYS:
        mate = ch ^ 1
        g.wait_ge(S.a1, 15 * 8)
        send([8 * mate + PARTNER[k], 8 * mate + k], [8 * ch + PARTNER[k], 8 * ch + TWIN[k]],
             [T.gath[i] for i in range(16)], T.part[:, par * W:(par + 1) * W], S.a2, 1)
        sent += 16

    v = g.vector
    v.wait_ge(S.v, 1)
    v.wait_ge(S.a2, 2 * 8)
    v.tensor_tensor(T.u[:], T.part[:, 0:W], T.part[:, W:2 * W], AluOpType.add).then_inc(S.v, 1)
    v.wait_ge(S.v, 2)
    v.tensor_tensor(T.ys[:], T.u[:], T.zero[:], AluOpType.max).then_inc(S.v, 1)
    g.sync.wait_ge(S.v, 3)
    g.sync.dma_start(T.y[:], T.ys[:]).then_inc(S.st, 16)
    g.sync.wait_ge(S.st, 16)
    g.wait_ge(S.sent, sent)
